import numpy as np
import ml_dtypes


def mxq(x, axis, fmt="e4m3"):
    dtype, down = {"e4m3": (ml_dtypes.float8_e4m3fn, 7), "e5m2": (ml_dtypes.float8_e5m2, 14)}[fmt]
    v = np.moveaxis(np.asarray(x, np.float32).astype(ml_dtypes.bfloat16).astype(np.float64), axis, -1)
    blocks = v.reshape(v.shape[:-1] + (-1, 32))
    amax = np.abs(blocks).max(-1, keepdims=True)
    byte = np.maximum(np.where(amax > 0, np.frexp(amax)[1] - 1 + 127, 0) - down, 1)
    scale = np.exp2(byte - 127.0)
    codes = (blocks / scale).astype(np.float32).astype(dtype).astype(np.float64)
    return np.moveaxis((codes * scale).reshape(v.shape), -1, axis)


WIDE = False


def mx_kscale(k, group=512):
    if not WIDE:
        return np.ones(k)
    levels = np.array([18, -18])
    if group != 512:
        return np.exp2(np.random.permutation(np.resize(levels, k // group))).repeat(group)
    if k % 512:
        return np.exp2(np.random.permutation(np.resize(levels, k // 32))).repeat(32)
    a = np.empty((k // 512, 16))
    for p in range(k // 512):
        a[p, :8] = np.random.permutation(np.resize(levels, 8))
        for g in range(8):
            far = levels[np.abs(levels - a[p, g]) >= 10]
            a[p, g + 8] = far[np.random.randint(len(far))]
    return np.exp2(a.ravel()).repeat(32)


def f64(x):
    return np.asarray(x).astype(np.float64)


def sigmoid(v):
    return 1.0 / (1.0 + np.exp(-v))


G, D, M, O, N = 4, 128, 128, 128, 512


def setup_inputs():
    n = np.random.standard_normal
    s_d = mx_kscale(D, 0)
    s_o = mx_kscale(O, 0)
    return {
        "x": (n((G, D, N)) * s_d[:, None]).astype(np.float32),
        "w1": (n((G, D, M)) / np.sqrt(D) / s_d[:, None]).astype(np.float32),
        "w2": (n((G, D, M)) / np.sqrt(D) / s_d[:, None]).astype(np.float32),
        "gn": (np.random.uniform(0.5, 2.0, (G, M, 1))).astype(np.float32),
        "wo": (n((G, O, M)) / np.sqrt(O) / s_o[:, None]).astype(np.float32),
        "dy": (n((G, O, N)) * s_o[:, None]).astype(np.float32),
        "old": (0.3 * n((G, M, N))).astype(np.float32),
    }


def reference(x, w1, w2, gn, wo, dy, old):
    w1q = mxq(f64(w1), 1, "e4m3")
    xq = mxq(f64(x), 1, "e4m3")
    z1 = w1q.transpose(0, 2, 1) @ xq
    w2q = mxq(f64(w2), 1, "e4m3")
    z2 = w2q.transpose(0, 2, 1) @ xq
    rm = np.sqrt(np.mean(np.square(z1), axis=-1, keepdims=True) + 0.01)
    woq = mxq(f64(wo), 1, "e4m3")
    dyq = mxq(f64(dy), 1, "e4m3")
    c0 = woq.transpose(0, 2, 1) @ dyq
    dnz = c0 * sigmoid(z2)
    drm = np.sum(dnz * f64(gn) * z1 / np.square(rm) * (-1.0), axis=-1, keepdims=True)
    dz1 = dnz * f64(gn) / rm + drm * 0.5 / np.sqrt(np.mean(np.square(z1), axis=-1, keepdims=True) + 0.01) / 512.0 * z1 * 2.0
    y = dz1 + f64(old)
    return y

@@ -1,0 +1,221 @@
+import math
+from contextlib import ExitStack
+
+import concourse.mybir as mybir
+
+G, D, M, N = 4, 128, 128, 512
+FLOPS = 3 * 2 * G * D * M * N
+
+F32 = mybir.dt.float32
+BF16 = mybir.dt.bfloat16
+U32 = mybir.dt.uint32
+U8 = mybir.dt.uint8
+FP8X4 = mybir.dt.float8_e4m3fn_x4
+ACT = mybir.ActivationFunctionType
+ALU = mybir.AluOpType
+
+P = 128
+PACK = 4
+ROWS = D // PACK
+EPS = 0.01
+HALF = N // 2
+QUARTER = N // 4
+X_SPLIT = 320
+
+
+def tile_rows_brownorm_kernel(tc, x, w1, w2, gn, wo, dy, old, out):
+    nc = tc.nc
+
+    with ExitStack() as ctx:
+        sb = ctx.enter_context(tc.tile_pool(name="sb", bufs=1))
+        ps = ctx.enter_context(tc.psum_pool(name="ps", bufs=1))
+        ctx.enter_context(tc.manual_schedule())
+
+        def tile(name, shape, dtype):
+            return sb.tile(shape, dtype, name=name, align_bytes=64)
+
+        def packed_rows(t):
+            return t.rearrange("g (p j) c -> (g p) j c", j=PACK)
+
+        def interleave(copy, dst, src):
+            copy(
+                out=dst.rearrange("p (c i) j -> p c j i", i=4),
+                in_=src.rearrange("p j (c i) -> p c j i", i=4),
+            )
+
+        def quantize(codes, scales, src):
+            nc.vector.quantize_mx(
+                out=codes.bitcast(FP8X4), scales=scales, in_=src.rearrange("p c j -> p (c j)")
+            )
+
+        def product(acc, g, w_codes, w_scales, a_codes, a_scales):
+            rows = slice(ROWS * g, ROWS * (g + 1))
+            nc.tensor.matmul_mx(
+                out=acc[:],
+                lhsT=w_codes[rows, :].bitcast(FP8X4),
+                lhsT_scale=w_scales[rows, :],
+                rhs=a_codes[rows, :].bitcast(FP8X4),
+                rhs_scale=a_scales[rows, :],
+                start=True,
+                stop=True,
+            )
+
+        w1_raw = tile("w1_raw", [P, PACK, M], F32)
+        w2_raw = tile("w2_raw", [P, PACK, M], F32)
+        wo_raw = tile("wo_raw", [P, PACK, M], F32)
+        x_raw = tile("x_raw", [P, PACK, N], F32)
+        dy_raw = [tile("dy_raw%d" % h, [P, PACK, HALF], F32) for h in range(2)]
+        old_sb = [tile("old%d" % g, [P, N], F32) for g in range(G)]
+        gn_rows = tile("gn_rows", [P, P], F32)
+        gn_cols = tile("gn_cols", [P, P], F32)
+        zero = tile("zero", [P, 2], F32)
+        half = tile("half", [P, 2], F32)
+        expo = tile("expo", [P, 2], F32)
+
+        nc.vector.memset(gn_rows[:], 0.0)
+        nc.gpsimd.memset(zero[:], 0.0)
+        nc.scalar.activation(out=half[:], in_=zero[:], func=ACT.Sigmoid)
+        nc.gpsimd.tensor_scalar(out=expo[:], in0=half[:], scalar1=-1.0, scalar2=0.0, op0=ALU.mult, op1=ALU.add)
+
+        nc.sync.dma_start(out=w1_raw[:], in_=packed_rows(w1))
+        nc.sync.dma_start(out=x_raw[:], in_=packed_rows(x))
+        nc.sync.dma_start(
+            out=gn_rows[0:P:32, :].rearrange("q (g i) -> q g i", i=32),
+            in_=gn.rearrange("g (q i) o -> q g (i o)", i=32),
+        )
+        nc.sync.dma_start(out=w2_raw[:], in_=packed_rows(w2))
+        nc.sync.dma_start(out=wo_raw[:], in_=packed_rows(wo))
+        for h in range(2):
+            nc.sync.dma_start(out=dy_raw[h][:], in_=packed_rows(dy)[:, :, h * HALF : (h + 1) * HALF])
+        for g in range(G):
+            nc.sync.dma_start(out=old_sb[g][:], in_=old[g])
+
+        w1_bf = tile("w1_bf", [P, M, PACK], BF16)
+        w1_codes = tile("w1_codes", [P, M], U32)
+        w1_scales = tile("w1_scales", [P, M], U8)
+        interleave(nc.vector.tensor_copy, w1_bf[:], w1_raw[:])
+        quantize(w1_codes[:], w1_scales[:], w1_bf[:])
+
+        x_bf = tile("x_bf", [P, N, PACK], BF16)
+        x_codes = tile("x_codes", [P, N], U32)
+        x_scales = tile("x_scales", [P, N], U8)
+        interleave(nc.vector.tensor_copy, x_bf[:, 0:HALF, :], x_raw[:, :, 0:HALF])
+        interleave(nc.vector.tensor_copy, x_bf[:, HALF:X_SPLIT, :], x_raw[:, :, HALF:X_SPLIT])
+        interleave(nc.scalar.copy, x_bf[:, X_SPLIT:N, :], x_raw[:, :, X_SPLIT:N])
+        for h in range(2):
+            cols = slice(h * HALF, (h + 1) * HALF)
+            quantize(x_codes[:, cols], x_scales[:, cols], x_bf[:, cols, :])
+
+        z1 = [ps.tile([P, N], F32, name="z1_%d" % g) for g in range(G)]
+        gate_then_c0 = [ps.tile([P, N], F32, name="zc_%d" % g) for g in range(G)]
+        for g in range(G):
+            product(z1[g], g, w1_codes, w1_scales, x_codes, x_scales)
+
+        w2o_bf = tile("w2o_bf", [P, 2 * M, PACK], BF16)
+        w2o_codes = tile("w2o_codes", [P, 2 * M], U32)
+        w2o_scales = tile("w2o_scales", [P, 2 * M], U8)
+        interleave(nc.vector.tensor_copy, w2o_bf[:, 0:M, :], w2_raw[:])
+        interleave(nc.vector.tensor_copy, w2o_bf[:, M : 2 * M, :], wo_raw[:])
+        nc.vector.transpose(out=gn_cols[:], in_=gn_rows[:])
+        quantize(w2o_codes[:], w2o_scales[:], w2o_bf[:])
+        for g in range(G):
+            product(gate_then_c0[g], g, w2o_codes[:, 0:M], w2o_scales[:, 0:M], x_codes, x_scales)
+
+        squares = tile("squares", [P, N], F32)
+        sumsq = [tile("sumsq%d" % pair, [P, 2], F32) for pair in range(2)]
+        total = [tile("total%d" % pair, [P, 2], F32) for pair in range(2)]
+        factor = [tile("factor%d" % pair, [P, 2, 2], F32) for pair in range(2)]
+        coef = [tile("coef%d" % pair, [P, 2, 2], F32) for pair in range(2)]
+        for pair in range(2):
+            nc.gpsimd.tensor_scalar(
+                out=factor[pair][:, 0, :],
+                in0=gn_cols[:, 64 * pair : 64 * (pair + 1) : 32],
+                scalar1=-math.sqrt(N),
+                scalar2=0.0,
+                op0=ALU.mult,
+                op1=ALU.add,
+            )
+        for pair in range(2):
+            for k in range(2):
+                nc.scalar.activation(
+                    out=squares[:], in_=z1[2 * pair + k][:], func=ACT.Square, accum_out=sumsq[pair][:, k : k + 1]
+                )
+            nc.gpsimd.tensor_scalar(
+                out=total[pair][:], in0=sumsq[pair][:], scalar1=N * EPS, scalar2=1.0, op0=ALU.add, op1=ALU.mult
+            )
+            nc.gpsimd.tensor_tensor(out=factor[pair][:, 1, :], in0=total[pair][:], in1=expo[:], op=ALU.pow)
+            nc.gpsimd.tensor_tensor(
+                out=coef[pair][:],
+                in0=factor[pair][:],
+                in1=factor[pair][:, 1:2, :].to_broadcast([P, 2, 2]),
+                op=ALU.mult,
+            )
+
+        gate = [tile("gate%d" % g, [P, N], F32) for g in range(G)]
+        for g in range(G):
+            nc.scalar.activation(out=gate[g][:], in_=gate_then_c0[g][:], func=ACT.Sigmoid)
+
+        dy_bf = tile("dy_bf", [P, N, PACK], BF16)
+        dy_codes = tile("dy_codes", [P, N], U32)
+        dy_scales = tile("dy_scales", [P, N], U8)
+        for h in range(2):
+            for q in range(2):
+                cols = slice(h * HALF + q * QUARTER, h * HALF + (q + 1) * QUARTER)
+                interleave(nc.vector.tensor_copy, dy_bf[:, cols, :], dy_raw[h][:, :, q * QUARTER : (q + 1) * QUARTER])
+            for q in range(2):
+                cols = slice(h * HALF + q * QUARTER, h * HALF + (q + 1) * QUARTER)
+                quantize(dy_codes[:, cols], dy_scales[:, cols], dy_bf[:, cols, :])
+        for g in range(G):
+            product(gate_then_c0[g], g, w2o_codes[:, M : 2 * M], w2o_scales[:, M : 2 * M], dy_codes, dy_scales)
+
+        neg_direct = [tile("neg_direct%d" % g, [P, N], F32) for g in range(G)]
+        partial = [tile("partial%d" % g, [P, N], F32) for g in range(G)]
+        result = [tile("result%d" % g, [P, N], F32) for g in range(G)]
+        slope = [tile("slope%d" % g, [P, 1], F32) for g in range(G)]
+        terms = tile("terms", [P, N], F32)
+
+        def direct_term(g):
+            nc.vector.scalar_tensor_tensor(
+                out=neg_direct[g][:],
+                in0=gate_then_c0[g][:],
+                scalar=coef[g // 2][:, 0, g % 2 : g % 2 + 1],
+                in1=gate[g][:],
+                op0=ALU.mult,
+                op1=ALU.mult,
+            )
+            nc.gpsimd.tensor_tensor(out=partial[g][:], in0=old_sb[g][:], in1=neg_direct[g][:], op=ALU.subtract)
+
+        def row_slope(g):
+            nc.vector.scalar_tensor_tensor(
+                out=terms[:],
+                in0=z1[g][:],
+                scalar=coef[g // 2][:, 1, g % 2 : g % 2 + 1],
+                in1=neg_direct[g][:],
+                op0=ALU.mult,
+                op1=ALU.mult,
+                accum_out=slope[g][:],
+            )
+
+        def finish(g):
+            nc.vector.scalar_tensor_tensor(
+                out=result[g][:],
+                in0=z1[g][:],
+                scalar=slope[g][:],
+                in1=partial[g][:],
+                op0=ALU.mult,
+                op1=ALU.add,
+            )
+            nc.sync.dma_start(out=out[g], in_=result[g][:])
+
+        direct_term(0)
+        direct_term(1)
+        row_slope(0)
+        row_slope(1)
+        finish(0)
+        direct_term(2)
+        finish(1)
+        direct_term(3)
+        row_slope(2)
+        row_slope(3)
+        finish(2)
+        finish(3)

@@ -20,7 +20,7 @@ ROWS = D // PACK
 EPS = 0.01
 HALF = N // 2
 QUARTER = N // 4
-X_SPLIT = 320
+X_SPLIT = 160
 
 
 def tile_rows_brownorm_kernel(tc, x, w1, w2, gn, wo, dy, old, out):
@@ -63,7 +63,7 @@ def tile_rows_brownorm_kernel(tc, x, w1, w2, gn, wo, dy, old, out):
         w1_raw = tile("w1_raw", [P, PACK, M], F32)
         w2_raw = tile("w2_raw", [P, PACK, M], F32)
         wo_raw = tile("wo_raw", [P, PACK, M], F32)
-        x_raw = tile("x_raw", [P, PACK, N], F32)
+        x_raw = [tile("x_raw%d" % h, [P, PACK, HALF], F32) for h in range(2)]
         dy_raw = [tile("dy_raw%d" % h, [P, PACK, HALF], F32) for h in range(2)]
         old_sb = [tile("old%d" % g, [P, N], F32) for g in range(G)]
         gn_rows = tile("gn_rows", [P, P], F32)
@@ -78,11 +78,12 @@ def tile_rows_brownorm_kernel(tc, x, w1, w2, gn, wo, dy, old, out):
         nc.gpsimd.tensor_scalar(out=expo[:], in0=half[:], scalar1=-1.0, scalar2=0.0, op0=ALU.mult, op1=ALU.add)
 
         nc.sync.dma_start(out=w1_raw[:], in_=packed_rows(w1))
-        nc.sync.dma_start(out=x_raw[:], in_=packed_rows(x))
         nc.sync.dma_start(
             out=gn_rows[0:P:32, :].rearrange("q (g i) -> q g i", i=32),
             in_=gn.rearrange("g (q i) o -> q g (i o)", i=32),
         )
+        for h in range(2):
+            nc.sync.dma_start(out=x_raw[h][:], in_=packed_rows(x)[:, :, h * HALF : (h + 1) * HALF])
         nc.sync.dma_start(out=w2_raw[:], in_=packed_rows(w2))
         nc.sync.dma_start(out=wo_raw[:], in_=packed_rows(wo))
         for h in range(2):
@@ -93,86 +94,131 @@ def tile_rows_brownorm_kernel(tc, x, w1, w2, gn, wo, dy, old, out):
         w1_bf = tile("w1_bf", [P, M, PACK], BF16)
         w1_codes = tile("w1_codes", [P, M], U32)
         w1_scales = tile("w1_scales", [P, M], U8)
+        factor = tile("factor", [P, 2, 8], F32)
         interleave(nc.vector.tensor_copy, w1_bf[:], w1_raw[:])
+        nc.vector.transpose(out=gn_cols[:], in_=gn_rows[:])
         quantize(w1_codes[:], w1_scales[:], w1_bf[:])
+        nc.vector.tensor_scalar(
+            out=factor[:, 0, 0:G], in0=gn_cols[:, 0:P:32], scalar1=-math.sqrt(N), scalar2=None, op0=ALU.mult
+        )
 
         x_bf = tile("x_bf", [P, N, PACK], BF16)
         x_codes = tile("x_codes", [P, N], U32)
         x_scales = tile("x_scales", [P, N], U8)
-        interleave(nc.vector.tensor_copy, x_bf[:, 0:HALF, :], x_raw[:, :, 0:HALF])
-        interleave(nc.vector.tensor_copy, x_bf[:, HALF:X_SPLIT, :], x_raw[:, :, HALF:X_SPLIT])
-        interleave(nc.scalar.copy, x_bf[:, X_SPLIT:N, :], x_raw[:, :, X_SPLIT:N])
         for h in range(2):
             cols = slice(h * HALF, (h + 1) * HALF)
+            interleave(nc.vector.tensor_copy, x_bf[:, h * HALF : h * HALF + X_SPLIT, :], x_raw[h][:, :, 0:X_SPLIT])
+            interleave(nc.scalar.copy, x_bf[:, h * HALF + X_SPLIT : (h + 1) * HALF, :], x_raw[h][:, :, X_SPLIT:HALF])
             quantize(x_codes[:, cols], x_scales[:, cols], x_bf[:, cols, :])
-
-        z1 = [ps.tile([P, N], F32, name="z1_%d" % g) for g in range(G)]
-        gate_then_c0 = [ps.tile([P, N], F32, name="zc_%d" % g) for g in range(G)]
-        for g in range(G):
-            product(z1[g], g, w1_codes, w1_scales, x_codes, x_scales)
 
         w2o_bf = tile("w2o_bf", [P, 2 * M, PACK], BF16)
         w2o_codes = tile("w2o_codes", [P, 2 * M], U32)
         w2o_scales = tile("w2o_scales", [P, 2 * M], U8)
-        interleave(nc.vector.tensor_copy, w2o_bf[:, 0:M, :], w2_raw[:])
+        interleave(nc.scalar.copy, w2o_bf[:, 0:M, :], w2_raw[:])
         interleave(nc.vector.tensor_copy, w2o_bf[:, M : 2 * M, :], wo_raw[:])
-        nc.vector.transpose(out=gn_cols[:], in_=gn_rows[:])
         quantize(w2o_codes[:], w2o_scales[:], w2o_bf[:])
-        for g in range(G):
-            product(gate_then_c0[g], g, w2o_codes[:, 0:M], w2o_scales[:, 0:M], x_codes, x_scales)
 
-        squares = tile("squares", [P, N], F32)
+        z1 = [ps.tile([P, N], F32, name="z1_%d" % g) for g in range(G)]
+        gate_then_c0 = [ps.tile([P, N], F32, name="zc_%d" % g) for g in range(G)]
+        squares = [tile("squares%d" % k, [P, N], F32) for k in range(2)]
         sumsq = [tile("sumsq%d" % pair, [P, 2], F32) for pair in range(2)]
         total = [tile("total%d" % pair, [P, 2], F32) for pair in range(2)]
-        factor = [tile("factor%d" % pair, [P, 2, 2], F32) for pair in range(2)]
         coef = [tile("coef%d" % pair, [P, 2, 2], F32) for pair in range(2)]
-        for pair in range(2):
-            nc.gpsimd.tensor_scalar(
-                out=factor[pair][:, 0, :],
-                in0=gn_cols[:, 64 * pair : 64 * (pair + 1) : 32],
-                scalar1=-math.sqrt(N),
-                scalar2=0.0,
-                op0=ALU.mult,
-                op1=ALU.add,
-            )
-        for pair in range(2):
-            for k in range(2):
-                nc.scalar.activation(
-                    out=squares[:], in_=z1[2 * pair + k][:], func=ACT.Square, accum_out=sumsq[pair][:, k : k + 1]
-                )
-            nc.gpsimd.tensor_scalar(
-                out=total[pair][:], in0=sumsq[pair][:], scalar1=N * EPS, scalar2=1.0, op0=ALU.add, op1=ALU.mult
-            )
-            nc.gpsimd.tensor_tensor(out=factor[pair][:, 1, :], in0=total[pair][:], in1=expo[:], op=ALU.pow)
-            nc.gpsimd.tensor_tensor(
-                out=coef[pair][:],
-                in0=factor[pair][:],
-                in1=factor[pair][:, 1:2, :].to_broadcast([P, 2, 2]),
-                op=ALU.mult,
-            )
-
         gate = [tile("gate%d" % g, [P, N], F32) for g in range(G)]
-        for g in range(G):
-            nc.scalar.activation(out=gate[g][:], in_=gate_then_c0[g][:], func=ACT.Sigmoid)
-
         dy_bf = tile("dy_bf", [P, N, PACK], BF16)
         dy_codes = tile("dy_codes", [P, N], U32)
         dy_scales = tile("dy_scales", [P, N], U8)
-        for h in range(2):
-            for q in range(2):
-                cols = slice(h * HALF + q * QUARTER, h * HALF + (q + 1) * QUARTER)
-                interleave(nc.vector.tensor_copy, dy_bf[:, cols, :], dy_raw[h][:, :, q * QUARTER : (q + 1) * QUARTER])
-            for q in range(2):
-                cols = slice(h * HALF + q * QUARTER, h * HALF + (q + 1) * QUARTER)
-                quantize(dy_codes[:, cols], dy_scales[:, cols], dy_bf[:, cols, :])
-        for g in range(G):
+
+        def values(g):
+            product(z1[g], g, w1_codes, w1_scales, x_codes, x_scales)
+
+        def gate_sums(g):
+            product(gate_then_c0[g], g, w2o_codes[:, 0:M], w2o_scales[:, 0:M], x_codes, x_scales)
+
+        def back_sums(g):
             product(gate_then_c0[g], g, w2o_codes[:, M : 2 * M], w2o_scales[:, M : 2 * M], dy_codes, dy_scales)
+
+        def sum_of_squares(g):
+            nc.scalar.activation(
+                out=squares[g % 2][:], in_=z1[g][:], func=ACT.Square, accum_out=sumsq[g // 2][:, g % 2 : g % 2 + 1]
+            )
+
+        def sigmoid_gate(g):
+            nc.scalar.activation(out=gate[g][:], in_=gate_then_c0[g][:], func=ACT.Sigmoid)
+
+        def inverse_root(pair):
+            nc.gpsimd.tensor_tensor(
+                out=factor[:, 1, 2 * pair : 2 * pair + 2], in0=total[pair][:], in1=expo[:], op=ALU.pow
+            )
+
+        def coefficients(pair):
+            cols = slice(2 * pair, 2 * pair + 2)
+            nc.vector.tensor_tensor(
+                out=coef[pair][:],
+                in0=factor[:, :, cols],
+                in1=factor[:, 1:2, cols].to_broadcast([P, 2, 2]),
+                op=ALU.mult,
+            )
+
+        def coefficients_on_scalar(pair):
+            for k in range(2):
+                g = 2 * pair + k
+                nc.scalar.activation(
+                    out=coef[pair][:, 0, k : k + 1],
+                    in_=factor[:, 1, g : g + 1],
+                    func=ACT.Copy,
+                    scale=factor[:, 0, g : g + 1],
+                )
+            nc.scalar.activation(out=coef[pair][:, 1, :], in_=factor[:, 1, 2 * pair : 2 * pair + 2], func=ACT.Square)
+
+        def dy_copy(q):
+            src = dy_raw[q // 2][:, :, (q % 2) * QUARTER : (q % 2 + 1) * QUARTER]
+            interleave(nc.vector.tensor_copy, dy_bf[:, q * QUARTER : (q + 1) * QUARTER, :], src)
+
+        def dy_quantize(q):
+            cols = slice(q * QUARTER, (q + 1) * QUARTER)
+            quantize(dy_codes[:, cols], dy_scales[:, cols], dy_bf[:, cols, :])
+
+        for g in (0, 1):
+            values(g)
+        for g in (0, 1):
+            gate_sums(g)
+        for g in (2, 3):
+            values(g)
+        for g in (0, 1):
+            sum_of_squares(g)
+        for g in (0, 1):
+            sigmoid_gate(g)
+        for g in (2, 3):
+            sum_of_squares(g)
+
+        dy_copy(0)
+        dy_copy(1)
+        dy_quantize(0)
+        dy_quantize(1)
+        dy_copy(2)
+        dy_copy(3)
+        dy_quantize(2)
+        nc.vector.tensor_scalar(out=total[0][:], in0=sumsq[0][:], scalar1=N * EPS, scalar2=None, op0=ALU.add)
+        dy_quantize(3)
+        inverse_root(0)
+        coefficients(0)
+
+        for g in (0, 1):
+            back_sums(g)
+        for g in (2, 3):
+            gate_sums(g)
+        sigmoid_gate(2)
+        nc.scalar.activation(out=total[1][:], in_=sumsq[1][:], func=ACT.Identity, bias=N * EPS)
+        sigmoid_gate(3)
+        for g in (2, 3):
+            back_sums(g)
 
         neg_direct = [tile("neg_direct%d" % g, [P, N], F32) for g in range(G)]
         partial = [tile("partial%d" % g, [P, N], F32) for g in range(G)]
         result = [tile("result%d" % g, [P, N], F32) for g in range(G)]
         slope = [tile("slope%d" % g, [P, 1], F32) for g in range(G)]
-        terms = tile("terms", [P, N], F32)
+        terms = [tile("terms%d" % k, [P, N], F32) for k in range(2)]
 
         def direct_term(g):
             nc.vector.scalar_tensor_tensor(
@@ -183,11 +229,13 @@ def tile_rows_brownorm_kernel(tc, x, w1, w2, gn, wo, dy, old, out):
                 op0=ALU.mult,
                 op1=ALU.mult,
             )
+
+        def add_old(g):
             nc.gpsimd.tensor_tensor(out=partial[g][:], in0=old_sb[g][:], in1=neg_direct[g][:], op=ALU.subtract)
 
         def row_slope(g):
             nc.vector.scalar_tensor_tensor(
-                out=terms[:],
+                out=terms[g % 2][:],
                 in0=z1[g][:],
                 scalar=coef[g // 2][:, 1, g % 2 : g % 2 + 1],
                 in1=neg_direct[g][:],
@@ -196,26 +244,34 @@ def tile_rows_brownorm_kernel(tc, x, w1, w2, gn, wo, dy, old, out):
                 accum_out=slope[g][:],
             )
 
-        def finish(g):
+        def finish(g, cols):
             nc.vector.scalar_tensor_tensor(
-                out=result[g][:],
-                in0=z1[g][:],
+                out=result[g][:, cols],
+                in0=z1[g][:, cols],
                 scalar=slope[g][:],
-                in1=partial[g][:],
+                in1=partial[g][:, cols],
                 op0=ALU.mult,
                 op1=ALU.add,
             )
-            nc.sync.dma_start(out=out[g], in_=result[g][:])
+            nc.sync.dma_start(out=out[g][:, cols], in_=result[g][:, cols])
 
+        whole = slice(0, N)
         direct_term(0)
+        add_old(0)
+        inverse_root(1)
+        coefficients_on_scalar(1)
         direct_term(1)
+        add_old(1)
         row_slope(0)
         row_slope(1)
-        finish(0)
+        finish(0, whole)
         direct_term(2)
-        finish(1)
+        add_old(2)
         direct_term(3)
+        add_old(3)
+        finish(1, whole)
         row_slope(2)
         row_slope(3)
-        finish(2)
-        finish(3)
+        finish(2, whole)
+        finish(3, slice(0, HALF))
+        finish(3, slice(HALF, N))

@@ -1,4 +1,3 @@
-import math
 from contextlib import ExitStack
 
 import concourse.mybir as mybir
@@ -17,10 +16,12 @@ ALU = mybir.AluOpType
 P = 128
 PACK = 4
 ROWS = D // PACK
+BLOCK = 32
 EPS = 0.01
 HALF = N // 2
 QUARTER = N // 4
-X_SPLIT = 160
+X_VECTOR_SHARE = 160
+PADDED_ROW = 8
 
 
 def tile_rows_brownorm_kernel(tc, x, w1, w2, gn, wo, dy, old, out):
@@ -69,57 +70,78 @@ def tile_rows_brownorm_kernel(tc, x, w1, w2, gn, wo, dy, old, out):
         gn_rows = tile("gn_rows", [P, P], F32)
         gn_cols = tile("gn_cols", [P, P], F32)
         zero = tile("zero", [P, 2], F32)
-        half = tile("half", [P, 2], F32)
-        expo = tile("expo", [P, 2], F32)
+        plus_half = tile("plus_half", [P, 2], F32)
+        minus_half = tile("minus_half", [P, 2], F32)
+        count = tile("count", [P, 1], F32)
+        root_n = tile("root_n", [P, 1], F32)
 
         nc.vector.memset(gn_rows[:], 0.0)
         nc.gpsimd.memset(zero[:], 0.0)
-        nc.scalar.activation(out=half[:], in_=zero[:], func=ACT.Sigmoid)
-        nc.gpsimd.tensor_scalar(out=expo[:], in0=half[:], scalar1=-1.0, scalar2=0.0, op0=ALU.mult, op1=ALU.add)
-
-        nc.sync.dma_start(out=w1_raw[:], in_=packed_rows(w1))
-        nc.sync.dma_start(
-            out=gn_rows[0:P:32, :].rearrange("q (g i) -> q g i", i=32),
-            in_=gn.rearrange("g (q i) o -> q g (i o)", i=32),
+        nc.scalar.activation(out=plus_half[:], in_=zero[:], func=ACT.Sigmoid)
+        nc.gpsimd.tensor_scalar(
+            out=minus_half[:], in0=plus_half[:], scalar1=-1.0, scalar2=0.0, op0=ALU.mult, op1=ALU.add
         )
+        nc.gpsimd.memset(count[:], float(N))
+        nc.gpsimd.tensor_tensor(out=root_n[:], in0=count[:], in1=plus_half[:, 0:1], op=ALU.pow)
+
         for h in range(2):
             nc.sync.dma_start(out=x_raw[h][:], in_=packed_rows(x)[:, :, h * HALF : (h + 1) * HALF])
+        nc.sync.dma_start(out=w1_raw[:], in_=packed_rows(w1))
+        nc.sync.dma_start(
+            out=gn_rows[0:P:BLOCK, :].rearrange("q (g i) -> q g i", i=BLOCK),
+            in_=gn.rearrange("g (q i) o -> q g (i o)", i=BLOCK),
+        )
         nc.sync.dma_start(out=w2_raw[:], in_=packed_rows(w2))
-        nc.sync.dma_start(out=wo_raw[:], in_=packed_rows(wo))
         for h in range(2):
             nc.sync.dma_start(out=dy_raw[h][:], in_=packed_rows(dy)[:, :, h * HALF : (h + 1) * HALF])
+        nc.sync.dma_start(out=wo_raw[:], in_=packed_rows(wo))
         for g in range(G):
             nc.sync.dma_start(out=old_sb[g][:], in_=old[g])
 
         w1_bf = tile("w1_bf", [P, M, PACK], BF16)
         w1_codes = tile("w1_codes", [P, M], U32)
         w1_scales = tile("w1_scales", [P, M], U8)
-        factor = tile("factor", [P, 2, 8], F32)
-        interleave(nc.vector.tensor_copy, w1_bf[:], w1_raw[:])
-        nc.vector.transpose(out=gn_cols[:], in_=gn_rows[:])
-        quantize(w1_codes[:], w1_scales[:], w1_bf[:])
-        nc.vector.tensor_scalar(
-            out=factor[:, 0, 0:G], in0=gn_cols[:, 0:P:32], scalar1=-math.sqrt(N), scalar2=None, op0=ALU.mult
-        )
-
+        factor = tile("factor", [P, 2, PADDED_ROW], F32)
         x_bf = tile("x_bf", [P, N, PACK], BF16)
         x_codes = tile("x_codes", [P, N], U32)
         x_scales = tile("x_scales", [P, N], U8)
-        for h in range(2):
+
+        def x_copy(h):
+            split = h * HALF + X_VECTOR_SHARE
+            interleave(nc.vector.tensor_copy, x_bf[:, h * HALF : split, :], x_raw[h][:, :, 0:X_VECTOR_SHARE])
+            interleave(nc.scalar.copy, x_bf[:, split : (h + 1) * HALF, :], x_raw[h][:, :, X_VECTOR_SHARE:HALF])
+
+        def x_quantize(h):
             cols = slice(h * HALF, (h + 1) * HALF)
-            interleave(nc.vector.tensor_copy, x_bf[:, h * HALF : h * HALF + X_SPLIT, :], x_raw[h][:, :, 0:X_SPLIT])
-            interleave(nc.scalar.copy, x_bf[:, h * HALF + X_SPLIT : (h + 1) * HALF, :], x_raw[h][:, :, X_SPLIT:HALF])
             quantize(x_codes[:, cols], x_scales[:, cols], x_bf[:, cols, :])
+
+        x_copy(0)
+        x_quantize(0)
+        x_copy(1)
+        interleave(nc.vector.tensor_copy, w1_bf[:, 0 : M // 2, :], w1_raw[:, :, 0 : M // 2])
+        interleave(nc.scalar.copy, w1_bf[:, M // 2 : M, :], w1_raw[:, :, M // 2 : M])
+        x_quantize(1)
+        quantize(w1_codes[:], w1_scales[:], w1_bf[:])
 
         w2o_bf = tile("w2o_bf", [P, 2 * M, PACK], BF16)
         w2o_codes = tile("w2o_codes", [P, 2 * M], U32)
         w2o_scales = tile("w2o_scales", [P, 2 * M], U8)
-        interleave(nc.scalar.copy, w2o_bf[:, 0:M, :], w2_raw[:])
-        interleave(nc.vector.tensor_copy, w2o_bf[:, M : 2 * M, :], wo_raw[:])
-        quantize(w2o_codes[:], w2o_scales[:], w2o_bf[:])
+        w2_cols = slice(0, M)
+        wo_cols = slice(M, 2 * M)
+        interleave(nc.scalar.copy, w2o_bf[:, w2_cols, :], w2_raw[:])
+        nc.vector.transpose(out=gn_cols[:], in_=gn_rows[:])
+        nc.vector.tensor_scalar(
+            out=factor[:, 0, 0:G],
+            in0=gn_cols[:, 0:P:BLOCK],
+            scalar1=root_n[:],
+            scalar2=-1.0,
+            op0=ALU.mult,
+            op1=ALU.mult,
+        )
+        quantize(w2o_codes[:, w2_cols], w2o_scales[:, w2_cols], w2o_bf[:, w2_cols, :])
 
         z1 = [ps.tile([P, N], F32, name="z1_%d" % g) for g in range(G)]
-        gate_then_c0 = [ps.tile([P, N], F32, name="zc_%d" % g) for g in range(G)]
+        z2_then_c0 = [ps.tile([P, N], F32, name="zc_%d" % g) for g in range(G)]
         squares = [tile("squares%d" % k, [P, N], F32) for k in range(2)]
         sumsq = [tile("sumsq%d" % pair, [P, 2], F32) for pair in range(2)]
         total = [tile("total%d" % pair, [P, 2], F32) for pair in range(2)]
@@ -133,10 +155,10 @@ def tile_rows_brownorm_kernel(tc, x, w1, w2, gn, wo, dy, old, out):
             product(z1[g], g, w1_codes, w1_scales, x_codes, x_scales)
 
         def gate_sums(g):
-            product(gate_then_c0[g], g, w2o_codes[:, 0:M], w2o_scales[:, 0:M], x_codes, x_scales)
+            product(z2_then_c0[g], g, w2o_codes[:, w2_cols], w2o_scales[:, w2_cols], x_codes, x_scales)
 
         def back_sums(g):
-            product(gate_then_c0[g], g, w2o_codes[:, M : 2 * M], w2o_scales[:, M : 2 * M], dy_codes, dy_scales)
+            product(z2_then_c0[g], g, w2o_codes[:, wo_cols], w2o_scales[:, wo_cols], dy_codes, dy_scales)
 
         def sum_of_squares(g):
             nc.scalar.activation(
@@ -144,14 +166,14 @@ def tile_rows_brownorm_kernel(tc, x, w1, w2, gn, wo, dy, old, out):
             )
 
         def sigmoid_gate(g):
-            nc.scalar.activation(out=gate[g][:], in_=gate_then_c0[g][:], func=ACT.Sigmoid)
+            nc.scalar.activation(out=gate[g][:], in_=z2_then_c0[g][:], func=ACT.Sigmoid)
 
         def inverse_root(pair):
             nc.gpsimd.tensor_tensor(
-                out=factor[:, 1, 2 * pair : 2 * pair + 2], in0=total[pair][:], in1=expo[:], op=ALU.pow
+                out=factor[:, 1, 2 * pair : 2 * pair + 2], in0=total[pair][:], in1=minus_half[:], op=ALU.pow
             )
 
-        def coefficients(pair):
+        def coefficients_on_vector(pair):
             cols = slice(2 * pair, 2 * pair + 2)
             nc.vector.tensor_tensor(
                 out=coef[pair][:],
@@ -171,47 +193,50 @@ def tile_rows_brownorm_kernel(tc, x, w1, w2, gn, wo, dy, old, out):
                 )
             nc.scalar.activation(out=coef[pair][:, 1, :], in_=factor[:, 1, 2 * pair : 2 * pair + 2], func=ACT.Square)
 
-        def dy_copy(q):
-            src = dy_raw[q // 2][:, :, (q % 2) * QUARTER : (q % 2 + 1) * QUARTER]
-            interleave(nc.vector.tensor_copy, dy_bf[:, q * QUARTER : (q + 1) * QUARTER, :], src)
+        def dy_copy(h, start, stop):
+            dst = dy_bf[:, h * HALF + start : h * HALF + stop, :]
+            interleave(nc.vector.tensor_copy, dst, dy_raw[h][:, :, start:stop])
 
-        def dy_quantize(q):
-            cols = slice(q * QUARTER, (q + 1) * QUARTER)
+        def dy_quantize(h, start, stop):
+            cols = slice(h * HALF + start, h * HALF + stop)
             quantize(dy_codes[:, cols], dy_scales[:, cols], dy_bf[:, cols, :])
 
-        for g in (0, 1):
+        first, second = (0, 1), (2, 3)
+        for g in first:
             values(g)
-        for g in (0, 1):
+        for g in first:
             gate_sums(g)
-        for g in (2, 3):
+        for g in second:
             values(g)
-        for g in (0, 1):
+        for g in first:
             sum_of_squares(g)
-        for g in (0, 1):
+        for g in first:
             sigmoid_gate(g)
-        for g in (2, 3):
+        for g in second:
             sum_of_squares(g)
+        nc.scalar.activation(out=total[1][:], in_=sumsq[1][:], func=ACT.Identity, bias=N * EPS)
 
-        dy_copy(0)
-        dy_copy(1)
-        dy_quantize(0)
-        dy_quantize(1)
-        dy_copy(2)
-        dy_copy(3)
-        dy_quantize(2)
+        dy_copy(0, 0, QUARTER)
+        dy_copy(0, QUARTER, HALF)
+        dy_quantize(0, 0, QUARTER)
+        dy_quantize(0, QUARTER, HALF)
+        dy_copy(1, 0, HALF)
+        interleave(nc.vector.tensor_copy, w2o_bf[:, wo_cols, :], wo_raw[:])
+        dy_quantize(1, 0, HALF)
         nc.vector.tensor_scalar(out=total[0][:], in0=sumsq[0][:], scalar1=N * EPS, scalar2=None, op0=ALU.add)
-        dy_quantize(3)
+        quantize(w2o_codes[:, wo_cols], w2o_scales[:, wo_cols], w2o_bf[:, wo_cols, :])
         inverse_root(0)
-        coefficients(0)
+        coefficients_on_vector(0)
+        inverse_root(1)
 
-        for g in (0, 1):
+        for g in first:
             back_sums(g)
-        for g in (2, 3):
+        for g in second:
             gate_sums(g)
         sigmoid_gate(2)
-        nc.scalar.activation(out=total[1][:], in_=sumsq[1][:], func=ACT.Identity, bias=N * EPS)
+        coefficients_on_scalar(1)
         sigmoid_gate(3)
-        for g in (2, 3):
+        for g in second:
             back_sums(g)
 
         neg_direct = [tile("neg_direct%d" % g, [P, N], F32) for g in range(G)]
@@ -223,14 +248,12 @@ def tile_rows_brownorm_kernel(tc, x, w1, w2, gn, wo, dy, old, out):
         def direct_term(g):
             nc.vector.scalar_tensor_tensor(
                 out=neg_direct[g][:],
-                in0=gate_then_c0[g][:],
+                in0=z2_then_c0[g][:],
                 scalar=coef[g // 2][:, 0, g % 2 : g % 2 + 1],
                 in1=gate[g][:],
                 op0=ALU.mult,
                 op1=ALU.mult,
             )
-
-        def add_old(g):
             nc.gpsimd.tensor_tensor(out=partial[g][:], in0=old_sb[g][:], in1=neg_direct[g][:], op=ALU.subtract)
 
         def row_slope(g):
@@ -255,23 +278,18 @@ def tile_rows_brownorm_kernel(tc, x, w1, w2, gn, wo, dy, old, out):
             )
             nc.sync.dma_start(out=out[g][:, cols], in_=result[g][:, cols])
 
-        whole = slice(0, N)
+        whole, left, right = slice(0, N), slice(0, HALF), slice(HALF, N)
         direct_term(0)
-        add_old(0)
-        inverse_root(1)
-        coefficients_on_scalar(1)
         direct_term(1)
-        add_old(1)
         row_slope(0)
         row_slope(1)
-        finish(0, whole)
         direct_term(2)
-        add_old(2)
+        finish(0, whole)
         direct_term(3)
-        add_old(3)
-        finish(1, whole)
         row_slope(2)
+        finish(1, whole)
+        finish(2, left)
         row_slope(3)
-        finish(2, whole)
-        finish(3, slice(0, HALF))
-        finish(3, slice(HALF, N))
+        finish(2, right)
+        finish(3, left)
+        finish(3, right)

from contextlib import ExitStack

import concourse.mybir as mybir

G, D, M, N = 4, 128, 128, 512
FLOPS = 3 * 2 * G * D * M * N

F32 = mybir.dt.float32
BF16 = mybir.dt.bfloat16
U32 = mybir.dt.uint32
U8 = mybir.dt.uint8
FP8X4 = mybir.dt.float8_e4m3fn_x4
ACT = mybir.ActivationFunctionType
ALU = mybir.AluOpType

P = 128
PACK = 4
ROWS = D // PACK
BLOCK = 32
EPS = 0.01
HALF = N // 2
QUARTER = N // 4
X_VECTOR_SHARE = 160
PADDED_ROW = 8


def tile_rows_brownorm_kernel(tc, x, w1, w2, gn, wo, dy, old, out):
    nc = tc.nc

    with ExitStack() as ctx:
        sb = ctx.enter_context(tc.tile_pool(name="sb", bufs=1))
        ps = ctx.enter_context(tc.psum_pool(name="ps", bufs=1))
        ctx.enter_context(tc.manual_schedule())

        def tile(name, shape, dtype):
            return sb.tile(shape, dtype, name=name, align_bytes=64)

        def packed_rows(t):
            return t.rearrange("g (p j) c -> (g p) j c", j=PACK)

        def interleave(copy, dst, src):
            copy(
                out=dst.rearrange("p (c i) j -> p c j i", i=4),
                in_=src.rearrange("p j (c i) -> p c j i", i=4),
            )

        def quantize(codes, scales, src):
            nc.vector.quantize_mx(
                out=codes.bitcast(FP8X4), scales=scales, in_=src.rearrange("p c j -> p (c j)")
            )

        def product(acc, g, w_codes, w_scales, a_codes, a_scales):
            rows = slice(ROWS * g, ROWS * (g + 1))
            nc.tensor.matmul_mx(
                out=acc[:],
                lhsT=w_codes[rows, :].bitcast(FP8X4),
                lhsT_scale=w_scales[rows, :],
                rhs=a_codes[rows, :].bitcast(FP8X4),
                rhs_scale=a_scales[rows, :],
                start=True,
                stop=True,
            )

        w1_raw = tile("w1_raw", [P, PACK, M], F32)
        w2_raw = tile("w2_raw", [P, PACK, M], F32)
        wo_raw = tile("wo_raw", [P, PACK, M], F32)
        x_raw = [tile("x_raw%d" % h, [P, PACK, HALF], F32) for h in range(2)]
        dy_raw = [tile("dy_raw%d" % h, [P, PACK, HALF], F32) for h in range(2)]
        old_sb = [tile("old%d" % g, [P, N], F32) for g in range(G)]
        gn_rows = tile("gn_rows", [P, P], F32)
        gn_cols = tile("gn_cols", [P, P], F32)
        zero = tile("zero", [P, 2], F32)
        plus_half = tile("plus_half", [P, 2], F32)
        minus_half = tile("minus_half", [P, 2], F32)
        count = tile("count", [P, 1], F32)
        root_n = tile("root_n", [P, 1], F32)

        nc.vector.memset(gn_rows[:], 0.0)
        nc.gpsimd.memset(zero[:], 0.0)
        nc.scalar.activation(out=plus_half[:], in_=zero[:], func=ACT.Sigmoid)
        nc.gpsimd.tensor_scalar(
            out=minus_half[:], in0=plus_half[:], scalar1=-1.0, scalar2=0.0, op0=ALU.mult, op1=ALU.add
        )
        nc.gpsimd.memset(count[:], float(N))
        nc.gpsimd.tensor_tensor(out=root_n[:], in0=count[:], in1=plus_half[:, 0:1], op=ALU.pow)

        for h in range(2):
            nc.sync.dma_start(out=x_raw[h][:], in_=packed_rows(x)[:, :, h * HALF : (h + 1) * HALF])
        nc.sync.dma_start(out=w1_raw[:], in_=packed_rows(w1))
        nc.sync.dma_start(
            out=gn_rows[0:P:BLOCK, :].rearrange("q (g i) -> q g i", i=BLOCK),
            in_=gn.rearrange("g (q i) o -> q g (i o)", i=BLOCK),
        )
        nc.sync.dma_start(out=w2_raw[:], in_=packed_rows(w2))
        for h in range(2):
            nc.sync.dma_start(out=dy_raw[h][:], in_=packed_rows(dy)[:, :, h * HALF : (h + 1) * HALF])
        nc.sync.dma_start(out=wo_raw[:], in_=packed_rows(wo))
        for g in range(G):
            nc.sync.dma_start(out=old_sb[g][:], in_=old[g])

        w1_bf = tile("w1_bf", [P, M, PACK], BF16)
        w1_codes = tile("w1_codes", [P, M], U32)
        w1_scales = tile("w1_scales", [P, M], U8)
        factor = tile("factor", [P, 2, PADDED_ROW], F32)
        x_bf = tile("x_bf", [P, N, PACK], BF16)
        x_codes = tile("x_codes", [P, N], U32)
        x_scales = tile("x_scales", [P, N], U8)

        def x_copy(h):
            split = h * HALF + X_VECTOR_SHARE
            interleave(nc.vector.tensor_copy, x_bf[:, h * HALF : split, :], x_raw[h][:, :, 0:X_VECTOR_SHARE])
            interleave(nc.scalar.copy, x_bf[:, split : (h + 1) * HALF, :], x_raw[h][:, :, X_VECTOR_SHARE:HALF])

        def x_quantize(h):
            cols = slice(h * HALF, (h + 1) * HALF)
            quantize(x_codes[:, cols], x_scales[:, cols], x_bf[:, cols, :])

        x_copy(0)
        x_quantize(0)
        x_copy(1)
        interleave(nc.vector.tensor_copy, w1_bf[:, 0 : M // 2, :], w1_raw[:, :, 0 : M // 2])
        interleave(nc.scalar.copy, w1_bf[:, M // 2 : M, :], w1_raw[:, :, M // 2 : M])
        x_quantize(1)
        quantize(w1_codes[:], w1_scales[:], w1_bf[:])

        w2o_bf = tile("w2o_bf", [P, 2 * M, PACK], BF16)
        w2o_codes = tile("w2o_codes", [P, 2 * M], U32)
        w2o_scales = tile("w2o_scales", [P, 2 * M], U8)
        w2_cols = slice(0, M)
        wo_cols = slice(M, 2 * M)
        interleave(nc.scalar.copy, w2o_bf[:, w2_cols, :], w2_raw[:])
        nc.vector.transpose(out=gn_cols[:], in_=gn_rows[:])
        nc.vector.tensor_scalar(
            out=factor[:, 0, 0:G],
            in0=gn_cols[:, 0:P:BLOCK],
            scalar1=root_n[:],
            scalar2=-1.0,
            op0=ALU.mult,
            op1=ALU.mult,
        )
        quantize(w2o_codes[:, w2_cols], w2o_scales[:, w2_cols], w2o_bf[:, w2_cols, :])

        z1 = [ps.tile([P, N], F32, name="z1_%d" % g) for g in range(G)]
        z2_then_c0 = [ps.tile([P, N], F32, name="zc_%d" % g) for g in range(G)]
        squares = [tile("squares%d" % k, [P, N], F32) for k in range(2)]
        sumsq = [tile("sumsq%d" % pair, [P, 2], F32) for pair in range(2)]
        total = [tile("total%d" % pair, [P, 2], F32) for pair in range(2)]
        coef = [tile("coef%d" % pair, [P, 2, 2], F32) for pair in range(2)]
        gate = [tile("gate%d" % g, [P, N], F32) for g in range(G)]
        dy_bf = tile("dy_bf", [P, N, PACK], BF16)
        dy_codes = tile("dy_codes", [P, N], U32)
        dy_scales = tile("dy_scales", [P, N], U8)

        def values(g):
            product(z1[g], g, w1_codes, w1_scales, x_codes, x_scales)

        def gate_sums(g):
            product(z2_then_c0[g], g, w2o_codes[:, w2_cols], w2o_scales[:, w2_cols], x_codes, x_scales)

        def back_sums(g):
            product(z2_then_c0[g], g, w2o_codes[:, wo_cols], w2o_scales[:, wo_cols], dy_codes, dy_scales)

        def sum_of_squares(g):
            nc.scalar.activation(
                out=squares[g % 2][:], in_=z1[g][:], func=ACT.Square, accum_out=sumsq[g // 2][:, g % 2 : g % 2 + 1]
            )

        def sigmoid_gate(g):
            nc.scalar.activation(out=gate[g][:], in_=z2_then_c0[g][:], func=ACT.Sigmoid)

        def inverse_root(pair):
            nc.gpsimd.tensor_tensor(
                out=factor[:, 1, 2 * pair : 2 * pair + 2], in0=total[pair][:], in1=minus_half[:], op=ALU.pow
            )

        def coefficients_on_vector(pair):
            cols = slice(2 * pair, 2 * pair + 2)
            nc.vector.tensor_tensor(
                out=coef[pair][:],
                in0=factor[:, :, cols],
                in1=factor[:, 1:2, cols].to_broadcast([P, 2, 2]),
                op=ALU.mult,
            )

        def coefficients_on_scalar(pair):
            for k in range(2):
                g = 2 * pair + k
                nc.scalar.activation(
                    out=coef[pair][:, 0, k : k + 1],
                    in_=factor[:, 1, g : g + 1],
                    func=ACT.Copy,
                    scale=factor[:, 0, g : g + 1],
                )
            nc.scalar.activation(out=coef[pair][:, 1, :], in_=factor[:, 1, 2 * pair : 2 * pair + 2], func=ACT.Square)

        def dy_copy(h, start, stop):
            dst = dy_bf[:, h * HALF + start : h * HALF + stop, :]
            interleave(nc.vector.tensor_copy, dst, dy_raw[h][:, :, start:stop])

        def dy_quantize(h, start, stop):
            cols = slice(h * HALF + start, h * HALF + stop)
            quantize(dy_codes[:, cols], dy_scales[:, cols], dy_bf[:, cols, :])

        first, second = (0, 1), (2, 3)
        for g in first:
            values(g)
        for g in first:
            gate_sums(g)
        for g in second:
            values(g)
        for g in first:
            sum_of_squares(g)
        for g in first:
            sigmoid_gate(g)
        for g in second:
            sum_of_squares(g)
        nc.scalar.activation(out=total[1][:], in_=sumsq[1][:], func=ACT.Identity, bias=N * EPS)

        dy_copy(0, 0, QUARTER)
        dy_copy(0, QUARTER, HALF)
        dy_quantize(0, 0, QUARTER)
        dy_quantize(0, QUARTER, HALF)
        dy_copy(1, 0, HALF)
        interleave(nc.vector.tensor_copy, w2o_bf[:, wo_cols, :], wo_raw[:])
        dy_quantize(1, 0, HALF)
        nc.vector.tensor_scalar(out=total[0][:], in0=sumsq[0][:], scalar1=N * EPS, scalar2=None, op0=ALU.add)
        quantize(w2o_codes[:, wo_cols], w2o_scales[:, wo_cols], w2o_bf[:, wo_cols, :])
        inverse_root(0)
        coefficients_on_vector(0)
        inverse_root(1)

        for g in first:
            back_sums(g)
        for g in second:
            gate_sums(g)
        sigmoid_gate(2)
        coefficients_on_scalar(1)
        sigmoid_gate(3)
        for g in second:
            back_sums(g)

        neg_direct = [tile("neg_direct%d" % g, [P, N], F32) for g in range(G)]
        partial = [tile("partial%d" % g, [P, N], F32) for g in range(G)]
        result = [tile("result%d" % g, [P, N], F32) for g in range(G)]
        slope = [tile("slope%d" % g, [P, 1], F32) for g in range(G)]
        terms = [tile("terms%d" % k, [P, N], F32) for k in range(2)]

        def direct_term(g):
            nc.vector.scalar_tensor_tensor(
                out=neg_direct[g][:],
                in0=z2_then_c0[g][:],
                scalar=coef[g // 2][:, 0, g % 2 : g % 2 + 1],
                in1=gate[g][:],
                op0=ALU.mult,
                op1=ALU.mult,
            )
            nc.gpsimd.tensor_tensor(out=partial[g][:], in0=old_sb[g][:], in1=neg_direct[g][:], op=ALU.subtract)

        def row_slope(g):
            nc.vector.scalar_tensor_tensor(
                out=terms[g % 2][:],
                in0=z1[g][:],
                scalar=coef[g // 2][:, 1, g % 2 : g % 2 + 1],
                in1=neg_direct[g][:],
                op0=ALU.mult,
                op1=ALU.mult,
                accum_out=slope[g][:],
            )

        def finish(g, cols):
            nc.vector.scalar_tensor_tensor(
                out=result[g][:, cols],
                in0=z1[g][:, cols],
                scalar=slope[g][:],
                in1=partial[g][:, cols],
                op0=ALU.mult,
                op1=ALU.add,
            )
            nc.sync.dma_start(out=out[g][:, cols], in_=result[g][:, cols])

        whole, left, right = slice(0, N), slice(0, HALF), slice(HALF, N)
        direct_term(0)
        direct_term(1)
        row_slope(0)
        row_slope(1)
        direct_term(2)
        finish(0, whole)
        direct_term(3)
        row_slope(2)
        finish(1, whole)
        finish(2, left)
        row_slope(3)
        finish(2, right)
        finish(3, left)
        finish(3, right)
